import numpy as np, ml_dtypes
CORES = [10,34,74,98]
N = 4
import mx_ref
BF = ml_dtypes.bfloat16
def gcols(t, e):
    v = np.concatenate([t.reshape(8, 16, -1, 4), np.zeros((8, 16, 1, 4), BF)], axis=2)
    return np.ascontiguousarray(np.stack([v[g][:, e[g]] for g in range(8)])).reshape(128, -1)
def tile(rs):
    return np.stack(rs, axis=2).reshape(128, -1).astype(BF)
def pick(q, e):
    c = np.concatenate([q[0].reshape(128, -1, 4), np.zeros((128, 1, 4), np.uint8)], axis=1); s = np.concatenate([q[1], np.ones((16, 1), np.uint8)], axis=1)
    return (np.ascontiguousarray(c[:, e].reshape(128, -1)), np.ascontiguousarray(s[:, e]))
def join(*qs):
    return (np.concatenate([q[0] for q in qs], axis=1), np.concatenate([q[1] for q in qs], axis=1))
def put(q, e, v):
    c, s = q[0].reshape(128, -1, 4).copy(), q[1].copy(); c[:, e] = v[0].reshape(128, -1, 4); s[:, e] = v[1]
    return (c.reshape(128, -1), s)
def pk(c, s):
    return (np.ascontiguousarray(c), mx_ref.live(s))
def emit(q):
    return q[0], q[1]
def packed(v, rng):
    q = [mx_ref.quantize(np.ascontiguousarray(v[r])) for r in range(N)]
    return np.stack([a for a, b in q]), np.stack([mx_ref.plane(b, rng) for a, b in q])
def values_of_codes():
    e, c = np.zeros((128, 128, 4), np.float32), np.zeros((128, 2, 4), np.uint8)
    e[np.arange(128), np.arange(128), 0] = 1
    c[:127, :, 0] = np.arange(256).reshape(2, 128).T[:127]
    return mx_ref.matmul(mx_ref.quantize(e.reshape(128, 512).astype(BF)), (c.reshape(128, 8), np.full((16, 2), 127, np.uint8))).T.reshape(-1).astype(np.float64)
CODE_VALUE, SCALE_VALUE = values_of_codes(), 2.0 ** (np.arange(256) - 127.0)
def decode(q):
    return (CODE_VALUE[q[0]].reshape(16, 8, -1, 4) * SCALE_VALUE[q[1]][:, None, :, None] + 0.0).reshape(128, -1).astype(np.float32)
def f(rng, *shape):
    return mx_ref.flush((rng.standard_normal(shape, dtype=np.float32) * np.exp2(rng.integers(-2, 3, shape[:-1] + (1,)))).astype(BF))
def wide(rng, *shape, cols=0):
    v = rng.standard_normal(shape, dtype=np.float32) * np.exp2(rng.integers(-12, 13, shape)).astype(np.float32)
    if cols: v *= np.repeat(np.exp2(rng.integers(-cols, cols + 1, shape[:-2] + (1, shape[-1] // 4))) * (rng.random(shape[:-2] + (1, shape[-1] // 4)) > 0.0625), 4, axis=-1).astype(np.float32)
    return mx_ref.flush(v.astype(BF))
C, A, B, E, F, R = 320, 128, 64, 64, 5, 3
STEP = [1, 2]
def order(p):
    return np.argsort(-(p[::16] + np.float32(0.0)), axis=1, kind="stable")
def gput(t, e, h):
    a, b = t.reshape(8, 16, -1, 4).copy(), h.reshape(8, 16, -1, 4)
    for g in range(8): a[g][:, e[g]] = b[g]
    return a.reshape(128, -1)
def big(v):
    v = v.astype(np.float32)
    v[np.abs(v) < np.float32(2.0 ** -16)] = 0
    return v.astype(BF)
def numbers_of(rng):
    return {"x": big(f(rng, N, 128, 4 * C)), "u": np.array(f(rng, N, 128, 512)), "v": np.array(f(rng, N, 128, 512))}
def layers(rng):
    return big(f(rng, N, 128, 2048)).reshape(N, 8, 16, 4, 8, 16, 4)
def apart(w, k):
    w[:, :, :k] = 0
    w[:, :, :, :, :, :k] = 0
    return w
def holding(w, k):
    w = apart(w, k).reshape(N, 128, 4, 128, 4)
    i = np.flatnonzero(np.arange(128) % 16 < k)
    for b in range(4): w[:, i, b, i, b] = 32
    return w
def weights(rng, w):
    c, p = packed(np.ascontiguousarray(w).reshape(N, 128, 2048), rng)
    return {"wc": c, "ws": p}
def signs(rng):
    return np.stack([rng.permutation(8) % 2 * 2.0 - 1.0 for r in range(N)])
def setup_inputs(rng):
    return {**numbers_of(rng), **weights(rng, layers(rng))}
def setup_inputs_ties(rng):
    d = numbers_of(rng)
    e = rng.permutation(N)
    x = d["x"].reshape(N, 8, 16, C, 4)
    for r in range(N):
        k = np.zeros(C, int) if r == e[0] else rng.permutation(C) % 3
        a = x[r][:, :8, :3].copy()
        a[:, :, 2] = 0
        x[r][:, :8] = a[:, :, k]
    x[e[1]] = 0
    u = d["u"].reshape(N, 8, 16, 128, 4)
    u[:, :, 8:, ::16] = 0
    return {"x": x.reshape(N, 128, 4 * C), "u": u.reshape(N, 128, 512), "v": d["v"], **weights(rng, holding(layers(rng), 8))}
def setup_inputs_near(rng):
    d = numbers_of(rng)
    x = np.zeros((N, 8, 16, C, 4), np.float32)
    u = d["u"].reshape(N, 128, 128, 4)
    u[:, :, ::16] = 0
    o, c = rng.permutation(N) % 4, signs(rng)
    upper = np.arange(C) // (C // 2)
    for r in range(N):
        i = (np.arange(C) + rng.integers(0, C, (8, 1))) % C
        if o[r] == 3: i = i % (C // 2) * 2 + upper
        s = (i + 1) // 2
        size = 1.0 if o[r] < 2 else 2.0 ** -4
        g = ((s[:, :, None] >> np.arange(8)) & 1) * np.exp2(np.arange(8) - 23.0) * size
        if o[r] < 2: x[r, :, 0, :, 0] = c[r][:, None]
        if o[r] == 3: x[r, :, 0, :, 0] = (8 + upper) * 2.0 ** -30
        x[r, :, 8] = g[:, :, :4]
        x[r, :, 9] = g[:, :, 4:]
        x[r, :, 10:] = rng.integers(4, 8, (8, 6, C, 4)) * 2.0 ** -20 * size
        k = 1.0 if o[r] == 0 else 2.0 ** -30
        for h in range(0, 128, 16):
            u[r, h, h, 0] = k
            u[r, h + 8:h + 10, h] = k
    w = (np.abs(layers(rng).astype(np.float32)) * np.float32(0.125)).astype(BF)
    return {"x": x.reshape(N, 128, 4 * C).astype(BF), "u": u.reshape(N, 128, 512), "v": d["v"], **weights(rng, holding(w, 10))}
def setup_inputs_huge(rng):
    d = numbers_of(rng)
    c = np.stack([rng.permutation(C) % 2 * 2.0 - 1.0 for r in range(N)])
    c[rng.permutation(N) < N // 2] = -1
    x = (0.6 + 0.2 * rng.random((N, 128, C, 4))) * np.where(c < 0, -2.0 ** 30, 2.0 ** 28)[:, None, :, None]
    u = d["u"].reshape(N, 128, 128, 4)
    a = 2.0 ** 30 * (1 - 0.25 * rng.random((N, 128, 8, 4))) * signs(rng)[:, None, :, None]
    u[:, :, ::16] = a.astype(np.float32).astype(BF)
    return {"x": x.astype(np.float32).reshape(N, 128, 4 * C).astype(BF), "u": u.reshape(N, 128, 512), "v": d["v"], **weights(rng, holding(layers(rng), 16))}
def setup_inputs_levels(rng):
    d = numbers_of(rng)
    x = d["x"].reshape(N, 8, 16, C, 4)
    x[:, :, :8] = 0
    x[:, :, 1, :, 0] = 1
    for r in range(N):
        n = rng.permutation(np.array([0, 1, B - 1, B, B + 1, C - A - B, C - A - max(B, A // 2), rng.integers(0, C - A - B + 1)]))
        way = rng.permutation(8)
        for g in range(8):
            k = rng.permutation(C)[:A]
            if way[g] == 0: k = np.arange(A)
            if way[g] == 1: k = np.arange(C - A, C)
            s = rng.integers(1, 8, C)
            s[k] = rng.integers(8, 16, A)
            rest = np.setdiff1d(np.arange(C), k)[B:]
            e = rng.permutation(rest)[:n[g]]
            s[e] = -s[e]
            x[r, g, 0, :, 0] = (s * 0.125).astype(np.float32).astype(BF)
    u = d["u"].reshape(N, 128, 128, 4)
    u[:, :, ::16] = 0
    for h in range(0, 128, 16): u[:, h, h, 0] = 1
    w = apart(layers(rng), 8)
    half = rng.permutation(N)[:N // 2]
    for g in range(8):
        w[:, g, 1, 0, g, 1, 0] = 64
        for r in half: w[r, g, 1, 0, g, 0, 0] = -0.5
    return {"x": x.reshape(N, 128, 4 * C), "u": u.reshape(N, 128, 512), "v": d["v"], **weights(rng, w)}
def setup_inputs_spread(rng):
    d = setup_inputs(rng)
    d["x"] = big(wide(rng, N, 128, 4 * C, cols=6))
    return d
def check_inputs(d):
    b = []
    for k in ("x", "u", "v"):
        a = np.abs(d[k].astype(np.float32))
        if not (np.isfinite(a).all() and ((a == 0) | (a >= 2.0 ** -30) & (a <= 2.0 ** 30)).all()): b.append("a value of " + k)
    none, least, most = [emit(mx_ref.quantize(np.full((128, 16), k, np.float32).astype(BF)))[1][0, 0] for k in (0.0, 2.0 ** -30, 2.0 ** 30)]
    for r in range(N):
        if ((d["wc"][r] == 0x7F) | (d["wc"][r] == 0xFF)).any(): b.append("wc: a code that is no number")
        s = mx_ref.live(d["ws"][r])
        if ((s != none) & ((s < least) | (s > most))).any(): b.append("ws: a scale out of range")
    return b
def reference(x, u, v, wc, ws):
    qu = [mx_ref.quantize(u[r]) for r in range(N)]
    lay = [pk(wc[r], ws[r]) for r in range(N)]
    kept = [np.concatenate([x[r], np.zeros((128, 4 * C * R), BF)], axis=1) for r in range(N)]
    level = np.zeros((N, 8, C), np.int64)
    border = [decode(mx_ref.quantize(np.ascontiguousarray(x[r - 1][:, 4 * (C - E):]))).astype(BF) for r in range(N)]
    for t in range(R):
        sent = []
        for r in range(N):
            had = level[r].copy()
            o = order(mx_ref.matmul(qu[r], mx_ref.quantize(gcols(kept[r], had * C + np.arange(C)))))
            going, others = o[:, :A], np.sort(o[:, A:], axis=1)
            low = np.argsort(np.take_along_axis(had, others, axis=1), axis=1, kind="stable")[:, :B]
            e = np.concatenate([going, np.take_along_axis(others, low, axis=1)], axis=1)
            l = np.take_along_axis(had, e, axis=1)
            q = (R + 1) * C + e // F
            for k in range(F - 1, 0, -1):
                found = (e % F >= k) & (np.take_along_axis(had, np.maximum(e - k, 0), axis=1) >= l)
                q = np.where(found, l * C + e - k, q)
            a = gcols(kept[r], l * C + e).astype(np.float32)
            b = gcols(np.concatenate([kept[r], border[r]], axis=1), q).astype(np.float32)
            z = mx_ref.quantize(((a + b) * np.float32(0.5)).astype(BF))
            h = tile([mx_ref.matmul(pick(lay[r], np.arange(128 * i, 128 * i + 128)), z) * np.float32(0.03125) for i in range(4)])
            kept[r] = gput(kept[r], (l + 1) * C + e, h)
            np.put_along_axis(level[r], e, l + 1, axis=1)
            sent.append(mx_ref.quantize(gcols(h, np.argsort(going, axis=1)[:, A - E:])))
        if t < R - 1: border = [decode(sent[r - STEP[t]]).astype(BF) for r in range(N)]
    y, ol = np.zeros((N, 128, C), np.float32), np.zeros((N, 8, C), np.float32)
    oc, osc = np.zeros((N, 128, 4 * C), np.uint8), np.zeros((N, 16, C), np.uint8)
    for r in range(N):
        q = mx_ref.quantize(gcols(kept[r], level[r] * C + np.arange(C)))
        y[r] = mx_ref.matmul(mx_ref.quantize(v[r]), q)
        ol[r] = level[r]
        oc[r], osc[r] = emit(q)
    return {"y": y, "ol": ol, "oc": oc, "osc": osc}

from concourse.mybir import dt, AluOpType, ActivationFunctionType

C, E, R = 320, 64, 3
STEP = [1, 1, 2]
XB = 128
HB = [448, 640, 832]
PLN = 1024
HUGE, BIG = 2.0 ** 90, 2.0 ** 20
F8, U8, BF, F32 = "float8_e4m3fn_x4", "uint8", "bfloat16", "float32"

SCRATCH = {}
for _n, _w in [("X0", 1280), ("X1", 1280), ("X2", 1280), ("X3", 1280), ("UB", 512), ("VB", 512), ("CT", 4096), ("BLK", 512),
               ("UPP", 512), ("EW", 520), ("ONES", 520), ("JG", 512), ("NG", 520), ("STP", 4096), ("STH", 3072), ("Z", 768), ("OWN", 768),
               ("TT", 512), ("DS", 320), ("SG", 2240), ("JK", 1280), ("T16", 320), ("EQ", 320), ("MK", 320), ("C0", 320), ("C1", 320),
               ("C16", 320), ("T4", 192), ("EQ4", 192), ("C4", 192), ("C5", 320), ("RS", 784)]:
    SCRATCH[_n] = ("sbuf", [128, _w], BF)
for _n, _w in [("D1", 320), ("HOLD", 320), ("CV", 320), ("PAY", 320), ("PL", 320), ("RT", 960), ("CI", 320), ("A", 672), ("KT", 1600),
               ("LT", 1280), ("CZ", 192), ("J128", 144), ("OLN", 320), ("RD", 320), ("YB", 320), ("SM", 1280)]:
    SCRATCH[_n] = ("sbuf", [128, _w], F32)
for _n, _w in [("U", 128), ("U2", 128), ("V", 128), ("W", 512), ("X0", 512), ("X1", 320), ("X2", 320), ("X3", 320), ("C", 1024), ("K", 896),
               ("N", 132), ("Z", 192), ("T0", 128), ("T1", 128)]:
    SCRATCH["q" + _n] = ("sbuf", [128, _w], F8)
    SCRATCH["s" + _n] = ("sbuf", [128, _w], U8)
SCRATCH["SI"] = ("sbuf", [128, 256], "int32")
SCRATCH["OF"] = ("sbuf", [128, 512], "uint16")
for _k in range(8):
    SCRATCH["P%d" % _k] = ("psum", [128, 512], F32)

SEMAPHORES = ["ev", "es", "et", "eg", "arr0", "arr1", "arr2", "sent"] + ["dma%d" % _k for _k in range(14)]
SEM_OF = {"v": "ev", "s": "es", "t": "et", "g": "eg"}


def vw(name, a, b, step=1):
    return (name, a, b, step)


def is_bank(v):
    return v[0][0] == "P" and v[0][1:].isdigit()


def cols(v):
    return frozenset([0]) if is_bank(v) else frozenset(range(v[1], v[2], v[3]))


def emit_all(ops, queues, T):
    touched, known, clock = {}, {q: {} for q in queues}, []
    waits, marked = [], set()
    for n, o in enumerate(ops):
        deps = set()
        acc = [(v, False) for v in o["r"]] + [(v, True) for v in o["w"]]
        for v, w in acc:
            c = cols(v)
            for m, c2, w2 in touched.get(v[0], []):
                same = ops[m]["q"] == o["q"] and ops[m]["tok"] is None
                if same and o["q"] == "t":
                    continue
                if (w or w2 or (is_bank(v) and not same)) and not c.isdisjoint(c2):
                    deps.add(m)
        mine = []
        if o["q"] is not None:
            k = known[o["q"]]
            for m in sorted(deps, reverse=True):
                key = ops[m]["q"] if ops[m]["tok"] is None else m
                if k.get(key, -1) >= m:
                    continue
                mine.append(m)
                marked.add(m)
                k[key] = m
                for kk, mm in clock[m].items():
                    if k.get(kk, -1) < mm:
                        k[kk] = mm
            clock.append(dict(k))
        else:
            clock.append({})
        waits.append(mine)
        for v, w in acc:
            touched.setdefault(v[0], []).append((n, cols(v), w))
    count, token = {}, {}
    for n, o in enumerate(ops):
        if o["tok"] is not None:
            token[n] = o["tok"]
        elif n in marked:
            count[o["q"]] = count.get(o["q"], 0) + 1
            token[n] = (SEM_OF[o["q"]], count[o["q"]])
    for n, o in enumerate(ops):
        if o["q"] is None:
            continue
        q = queues[o["q"]]
        for m in waits[n]:
            q.wait_ge(T.sem[token[m][0]], token[m][1])
        ins = o["f"](q)
        if o["dma"]:
            ins.then_inc(T.sem[o["tok"][0]], 16)
        elif o["tok"] is None and n in marked:
            ins.then_inc(T.sem[token[n][0]], 1)
    for n, o in enumerate(ops):
        if o["dma"] and n not in marked:
            queues[o["q"]].wait_ge(T.sem[o["tok"][0]], 16)


def rank_program(g, core, T, topo):
    rank = T.rank_of(core)
    if rank is None:
        return
    n_ranks = len(T.cores)
    Op, Act = AluOpType, ActivationFunctionType
    ops, used = [], {"SM": 0, "SI": 0, "OF": 0, "dma": 0, "sent": 0}

    def small(buf, n):
        a = used[buf]
        used[buf] = a + n + n % 2
        return vw(buf, a, a + n)

    def smalls(buf, *ns):
        return [small(buf, n) for n in ns]

    def part(v, a, b, step=1):
        return vw(v[0], v[1] + a, v[1] + b, step)

    def ap(v):
        if isinstance(v, (int, float)) or v is None:
            return v
        if v[0] == "ind":
            return ap(v[1]).indirect(ap(v[2]))
        return T[v[0]][:, v[1]:v[2]] if v[3] == 1 else T[v[0]][:, v[1]:v[2]:v[3]]

    def views(*vs):
        out = []
        for v in vs:
            if isinstance(v, tuple):
                out += [v[1], v[2]] if v[0] == "ind" else [v]
        return out

    def rec(q, r, w, f, tok=None, is_dma=False):
        ops.append({"q": q, "r": views(*r), "w": w, "f": f, "tok": tok, "dma": is_dma})

    def ind(win, off):
        return ("ind", win, off)

    def ts(out, a, s1, o1, s2=None, o2=None):
        if o2 is None:
            rec("v", [a, s1], [out], lambda q: q.tensor_scalar(ap(out), ap(a), ap(s1), None, o1))
        else:
            rec("v", [a, s1, s2], [out], lambda q: q.tensor_scalar(ap(out), ap(a), ap(s1), ap(s2), o1, o2))

    def tt(out, a, b, o):
        rec("v", [a, b], [out], lambda q: q.tensor_tensor(ap(out), ap(a), ap(b), o))

    def cp(out, a):
        rec("v", [a], [out], lambda q: q.tensor_copy(ap(out), ap(a)))

    def scatter(win, off, a):
        rec("v", [a, off], [win], lambda q: q.tensor_copy(ap(ind(win, off)), ap(a)))

    def scan(out, d0, d1, init, o0, o1):
        rec("v", [d0, d1], [out], lambda q: q.tensor_tensor_scan(ap(out), ap(d0), ap(d1), init, o0, o1))

    def fill(out, val):
        rec("v", [], [out], lambda q: q.memset(ap(out), val))

    def act(out, a, func, bias=0.0, scale=1.0, accum=None):
        if accum is None:
            rec("s", [a, bias], [out], lambda q: q.activation(ap(out), ap(a), func, bias=ap(bias), scale=scale))
        else:
            rec("s", [a, bias], [out, accum], lambda q: q.activation(ap(out), ap(a), func, bias=ap(bias), scale=scale, accum_out=ap(accum)))

    def lin(out, a, scale, bias):
        act(out, a, Act.Identity, bias=bias, scale=scale)

    def quant(name, a, b, tile):
        qv, sv = vw("q" + name, a, b), vw("s" + name, a, b)
        rec("v", [tile], [qv, sv], lambda q: q.quantize_mx(ap(qv), ap(sv), ap(tile)))

    def mm(bank, left, la, right, ra, n, start=True, stop=True):
        o, a, b = vw("P%d" % bank, 0, n), vw("q" + left, la, la + 128), vw("s" + left, la, la + 128)
        c, d = vw("q" + right, ra, ra + n), vw("s" + right, ra, ra + n)
        rec("t", [a, b, c, d], [o], lambda q: q.matmul_mx(ap(o), ap(a), ap(b), ap(c), ap(d), start, stop))

    def iota(out, pattern, base, mult=0):
        if out[0] == "SI":
            rec("g", [], [out], lambda q: q.iota(ap(out), pattern, base, mult))
        else:
            rec("g", [], [out], lambda q: q.iota(ap(out), pattern, base, mult, allow_small_or_imprecise_dtypes=True))

    def sel(out, a, pattern, o, base, mult):
        rec("g", [a], [out], lambda q: q.affine_select(ap(out), ap(a), pattern, o, 0.0, base, mult))

    def dma(q, r, w, out, a):
        tok = ("dma%d" % used["dma"], 16)
        used["dma"] += 1
        rec(q, r, w, lambda e: e.dma_start(out, a), tok, True)

    def lanes(src, dst):
        e = topo.engines(src, dst)
        return [sum(1 << k for k in e[0:len(e):2]), sum(1 << k for k in e[1:4:2])], len(e[0:len(e):2]) + len(e[1:4:2])

    def send(k, name, a):
        dst = T.cores[(rank + STEP[k]) % n_ranks]
        rid, pid = topo.addr(dst)[:2]
        masks, n = lanes(core, dst)
        used["sent"] += n
        qs, ss = vw("q" + name, a, a + E), vw("s" + name, a, a + E)
        qd, sd = vw("qX0", C + E * k, C + E * k + E), vw("sX0", C + E * k, C + E * k + E)
        sem = T.sem["arr%d" % k]
        rec("g", [qs], [], lambda q: q.remote_dma(ap(qd).bitcast(dt.uint8), ap(qs).bitcast(dt.uint8), sem, T.sem.sent, pid, rid, masks[0]),
            ("sent", 0))
        rec("g", [ss], [], lambda q: q.remote_dma(ap(sd), ap(ss), sem, T.sem.sent, pid, rid, masks[1]), ("sent", 0))

    def unpack(k):
        src = T.cores[(rank - STEP[k]) % n_ranks]
        rec(None, [], [vw("qX0", C + E * k, C + E * k + E), vw("sX0", C + E * k, C + E * k + E)], None, ("arr%d" % k, lanes(src, core)[1]))
        for b in range(4):
            mm(4 + b, "K", 128 * (3 + b), "X0", C + E * k - E, 128)
        for b in range(4):
            act(vw("STH", b, 4 * E, 4), vw("P%d" % (4 + b), E, 2 * E), Act.Copy, scale=0.5)

    def plane(b, a, n):
        return vw("STP", PLN * b + a, PLN * b + a + n)

    tiles = [0, 320, 576, 768, 896]

    def row(m):
        c0, e = (tiles[0], 20 - m) if m >= 17 else (tiles[1], 16 - m) if m >= 13 else (tiles[4 - (m - 1) // 4], (m - 1) % 4)
        return vw("CT", 4 * c0 + e, 4 * (c0 + 16 * m), 4)

    def own_score(m):
        return vw("HOLD", 16 * m + 15, 16 * m + 16)

    X = [vw("X%d" % t, 0, 4 * C) for t in range(R + 1)]
    pi, ai, gi_, a4i, ti, qj, qi, vi, ei, ri = smalls("SI", 1, 1, 1, 1, 1, 20, 20, 48, 48, 48)
    pa, pg, pa4, pt, kka, n4, pt2, w1, w2, w3, w4, w5, w6 = smalls("SM", *[1] * 13)
    m16, kk, b1, base, rk, g1, bgo, mn1, mn2, place, chk, npt, ch3, kc, uk, p02, sgn, r5, rr, lastb, kc0, q1 = smalls("SM", *[20] * 22)
    wsum, wpre, ot4, kb, gsum, kraw, kold, knew = smalls("SM", 23, 16, 16, 4, 4, 40, 40, 40)
    pen, cum, tmx, thr, zeros = smalls("SM", *[60] * 5)
    ptr, lv = smalls("SM", *[20] * (R + 1)), smalls("SM", *[20] * (R + 1))
    ou, ow, owp, pu, oo, ord_, og, ot, ox, olv, okey = smalls("OF", 8, 1, 1, 20, 48, 48, 20, 16, 20, 20, 40)
    bc, iw = part(kold, 20, 40), lv[0]

    def count(c):
        act(vw("JK", C * c, C * c + C), vw("OLN", 0, C), Act.Sign, bias=part(kb, c, c + 1), accum=part(gsum, c, c + 1))

    def keys(l):
        act(vw("A", 336 * l - 335, 336 * l - 15), ind(vw("KT", 0, 1600), part(okey, 20 * l - 20, 20 * l)), Act.Copy)

    def nearest(l):
        scan(vw("RT", C * l, C * l + C), vw("C5", 0, C), vw("A", 336 * l - 336, 336 * l - 16), 0.0, Op.mult, Op.max)

    dma("s", [], [vw("UB", 0, 512)], T.UB[:], T.u[:])
    dma("y", [], [X[0]], T.X0[:], T.x[:])
    dma("y", [X[0]], [vw("qW", 0, 512)], T.qW[:].bitcast(dt.uint8), T.wc[:])
    dma("y", [], [vw("sW", 0, 512)], T.sW[:], T.ws[:])
    dma("y", [], [vw("VB", 0, 512)], T.VB[:], T.v[:])

    iota(pi, [[0, 1]], 0, 1)
    iota(m16, [[16, 20]], 0)
    iota(vw("T16", 0, C), [[0, 20], [1, 16]], 0)
    iota(vw("JG", 0, 512), [[1, 8], [0, 64]], 0)
    fill(vw("ONES", 0, 520), 1.0)
    fill(zeros, 0.0)
    fill(vw("A", 0, 337, 336), float(E))
    ts(ai, pi, 15, Op.bitwise_and)
    ts(gi_, pi, 4, Op.logical_shift_right)
    ts(a4i, pi, 2, Op.logical_shift_right, 3, Op.bitwise_and)
    ts(ti, pi, 3, Op.bitwise_and)
    cp(ou, part(m16, 0, 8))
    cp(pa, ai)
    cp(pg, gi_)
    cp(pa4, a4i)
    cp(pt, ti)
    for a, b in [(272, 320), (528, 576), (720, 768), (848, 896), (912, 1024)]:
        fill(vw("CT", 4 * a, 4 * b), 0.0)
    ts(iw, m16, pa, Op.add)
    ts(w1, pa4, 3.0, Op.is_equal, -32.0, Op.mult)
    ts(w2, pa4, -32.0, Op.mult, 223.0, Op.add)
    ts(w4, pa4, 3.0, Op.is_equal, 1000.0, Op.mult)
    ts(w5, pa4, -64.0, Op.mult, 223.0, Op.add)
    ts(vw("EQ", 0, C), vw("T16", 0, C), pa, Op.is_equal)
    ts(qj, iw, 205.0, Op.mult)
    ts(w3, pt, 192.0, Op.mult, w2, Op.add)
    ts(w6, pt, 192.0, Op.mult, w5, Op.add)
    ts(qi, qj, 10, Op.logical_shift_right)
    ts(ow, w3, w1, Op.add, 768.0, Op.min)
    ts(owp, w6, w4, Op.add, 768.0, Op.min)
    act(vw("NG", 0, 520), vw("ONES", 0, 520), Act.Copy, scale=0.0)
    act(vw("TT", 4 * E, 8 * E), vw("ONES", 0, 4 * E), Act.Copy, scale=0.0)
    act(vw("C1", 0, C), vw("T16", 0, C), Act.Sign)
    act(vw("UPP", 0, 512), vw("ONES", 0, 512), Act.Copy, scale=0.0)
    lin(vw("MK", 0, C), vw("EQ", 0, C), 2 * HUGE, -HUGE)
    lin(vw("C0", 0, C), vw("C1", 0, C), 2 * HUGE, -HUGE)
    quant("U", 0, 128, vw("UB", 0, 512))
    ts(r5, qi, -5.0, Op.mult)
    ts(q1, qi, 1.0, Op.add)
    rec("v", [vw("qU", 0, 128), ou], [vw("qU2", 0, 128)],
        lambda q: q.tensor_copy(T.qU2[:, 0:128].bitcast(dt.uint32), T.qU[:, 0:128].bitcast(dt.uint32).indirect(ap(ou))))
    rec("s", [vw("sU", 0, 128), ou], [vw("sU2", 0, 128)], lambda q: q.activation(T.sU2[:, 0:128], T.sU[:, 0:128].indirect(ap(ou)), Act.Copy))
    sel(vw("EW", 0, 516), vw("ONES", 0, 516), [[1, 516]], Op.is_equal, -3, -4)
    tt(rr, r5, iw, Op.add)
    ts(vw("BLK", 0, 512), vw("JG", 0, 512), pg, Op.is_equal)
    ts(lastb, rr, 4.0, Op.is_equal, BIG, Op.mult)
    ts(kc0, rr, 384.0, Op.mult, -384.0, Op.add)
    quant("K", 0, 128, vw("BLK", 0, 512))
    act(vw("RS", 768, 784), vw("ONES", 0, 16), Act.Copy, scale=-192.0)
    lin(kka, pa, 1023.0, -15473.0)
    lin(vw("C16", 0, C), vw("EQ", 0, C), -BIG, 1024.0)
    lin(kk, m16, 1.0, kka)
    act(vw("STH", 4 * E, 4 * (E + C)), X[0], Act.Copy, scale=0.5)

    def constants_on_gpsimd():
        sel(vw("JG", 0, 512, 4), vw("BLK", 0, 512, 4), [[1, 128]], Op.is_ge, 0, -1)
        sel(vw("UPP", 0, 512, 4), vw("BLK", 0, 512, 4), [[-1, 128]], Op.is_gt, 0, 1)
        iota(vw("T4", 0, 192), [[0, 48], [1, 4]], 0)
        iota(vw("PAY", 0, C), [[8193, C]], XB - 1 - 2 ** 22)
        iota(vw("RT", 0, C), [[1, C]], XB - 1)
        iota(vw("RT", 0, C, 5), [[1, E]], E)
        iota(vw("J128", 0, 144), [[1, 144]], 0)
        iota(vw("KT", 0, 64), [[1, 64]], E)
        iota(vw("KT", 64, 1600), [[1024, 4], [1, 384]], 1024 + HB[0])
        sel(vw("C5", 0, C), vw("ONES", 0, C), [[0, E], [1, 5]], Op.is_gt, 0, 0)
        iota(vw("CI", 0, C), [[8192, C]], -2 ** 22)

    def constants_on_scalar():
        lin(vw("C4", 0, 192), vw("EQ4", 0, 192), -2.0 ** 27, 2.0 ** 22)
        lin(n4, pa4, 2.0 ** 22, -2 * 2.0 ** 22)
        lin(pt2, pt, 1.0, -4.0 * E)
        lin(ptr[0], iw, 1.0, float(XB))
        lin(kb, part(iw, 0, 4), -1.0, -64.5)
        for b in range(4):
            act(plane(b, XB, C), vw("X0", b, 4 * C, 4), Act.Copy)
            if b == 1:
                lin(vw("PAY", 0, C, 5), vw("RT", 0, C, 5), 40961.0, -64.0 * 40960 - 2.0 ** 22)

    for t in range(R):
        nl = t + 1
        more = t < R - 1
        quant("X%d" % t, 0, C, X[t])
        mm(0, "U2", 0, "X%d" % t, 0, C)
        mm(1, "U2", 0, "X%d" % t, 0, C)
        if t == 0:
            send(0, "X0", C - E)
            constants_on_gpsimd()
            tt(bc, q1, lastb, Op.min)
            tt(kc, kc0, lastb, Op.subtract)
            for b in range(2):
                quant("K", 128 * (3 + b), 128 * (4 + b), vw("EW", 3 - b, 515 - b))
        else:
            for b in range(4):
                act(vw("TT", b, 4 * E, 4), ind(X[t], part(ot, 4 * b, 4 * b + 4)), Act.Copy)
            if t == 2:
                keys(2)
            nearest(1)
        tt(vw("D1", 208, C), vw("P0", 208, C), vw("MK", 208, C), Op.min)
        scan(vw("HOLD", 208, C), vw("C0", 208, C), vw("D1", 208, C), -HUGE, Op.min, Op.max)
        tt(vw("D1", 0, 208), vw("P0", 0, 208), vw("MK", 0, 208), Op.min)
        if t > 0:
            quant("T%d" % (t - 1), 0, 128, vw("TT", 0, 512))
            send(t, "T%d" % (t - 1), 0)
        scan(vw("HOLD", 0, 208), vw("C0", 0, 208), vw("D1", 0, 208), -HUGE, Op.min, Op.max)
        if t == 1:
            iota(vw("LT", 0, 1280), [[1, 4], [0, C]], 0)
        high = list(range(19, 12, -1))
        for k in range(len(high) + 1):
            if k < len(high):
                m = high[k]
                act(vw("SG", C * k, C * k + 16 * m), vw("P1", 0, 16 * m), Act.Sign, bias=own_score(m), scale=-1.0)
            if k > 0:
                m = high[k - 1]
                act(row(m), vw("SG", C * (k - 1), C * (k - 1) + 16 * m), Act.Relu, accum=part(wsum, m + 3, m + 4))
        tt(vw("CT", 0, 4 * C, 4), vw("HOLD", 0, C), vw("P0", 0, C), Op.is_ge)
        for m in range(12, 0, -1):
            ts(row(m), vw("P0", 0, 16 * m), own_score(m), Op.is_lt)
        scan(vw("DS", 0, C), vw("C1", 0, C), vw("CT", 0, 4 * C, 4), 0.0, Op.mult, Op.add)
        quant("C", 0, 320, vw("CT", 0, 1280))
        mm(2, "K", 0, "C", 0, 320, True, False)
        for e in range(4):
            scan(vw("RS", 192 * e, 192 * e + 192), vw("CT", 4 * 576 + e, 4 * 960, 8), vw("CT", 4 * 577 + e, 4 * 960, 8), -192.0, Op.add, Op.add)
        last = 1024 if t == 0 else 960
        quant("C", 576, last, vw("CT", 4 * 576, 4 * last))
        mm(2, "K", 0, "C", 576, 192, False, False)
        mm(2, "K", 0, "C", 768, 128, False, False)
        mm(2, "K", 0, "C", 896, 128, False, False)
        cp(wpre, ind(vw("RS", 0, 784), owp))
        tt(b1, vw("DS", 15, C, 16), kk, Op.subtract)
        tt(part(wsum, 0, 16), ind(vw("RS", 0, 784), ow), wpre, Op.subtract)
        if t == 0:
            ts(vw("EQ4", 0, 192), vw("T4", 0, 192), pa4, Op.is_equal)
        if t == 2:
            nearest(2)
        quant("C", 320, 576, vw("CT", 1280, 4 * 576))
        mm(2, "K", 0, "C", 320, 256, False, True)
        tt(base, part(wsum, 3, 23), b1, Op.add)
        if t == 0:
            constants_on_scalar()
            quant("K", 128, 256, vw("JG", 0, 512))
            quant("K", 256, 384, vw("UPP", 0, 512))
        else:
            for l in range(nl):
                tt(part(thr, 20 * l, 20 * l + 20), base, part(pen, 20 * l, 20 * l + 20), Op.add)
            for b in range(4):
                act(vw("STH", 4 * (HB[t - 1] - E) + b, 4 * (HB[t] - E), 4), plane(b, HB[t - 1], 192), Act.Copy, scale=0.5)
            act(vw("RD", 0, C), ind(vw("RT", 0, C * nl), olv), Act.Copy)
            unpack(t)
        scan(vw("CV", 0, C), vw("C16", 0, C), vw("P2", 0, C), 0.0, Op.add, Op.max)
        lists = nl + 1 if more else nl
        for l in range(lists):
            flags = vw("NG", 8 + 160 * l, 8 + 160 * l + 160, 8)
            if l == nl or t == 0:
                tt(flags, vw("CV", 15, C, 16), base, Op.is_lt if l == nl else Op.is_ge)
            else:
                tt(flags, vw("CV", 15, C, 16), part(thr, 20 * l, 20 * l + 20), Op.is_ge)
        tt(rk, vw("CV", 15, C, 16), base, Op.subtract)
        quant("N", 0, 130, vw("NG", 0, 520))
        mm(3, "K", 128, "N", 2, 128, True, False)
        mm(3, "K", 256, "N", 0, 128, False, True)
        ts(g1, rk, -1000.0, Op.mult, 320.0, Op.min)
        if t > 0:
            scan(vw("PAY", 0, C), vw("RD", 0, C), vw("CI", 0, C), 0.0, Op.max, Op.add)
        else:
            for b in (2, 3):
                quant("K", 128 * (3 + b), 128 * (4 + b), vw("EW", 3 - b, 515 - b))
            unpack(0)
        tt(bgo, g1, rk, Op.add)
        scan(part(cum, 0, 20 * lists), part(zeros, 0, 20 * lists), vw("P3", 0, 40 * lists, 2), 192.0, Op.add, Op.subtract)
        low = part(cum, 0, 20)
        if t > 0:
            tt(part(tmx, 0, 20 * nl), part(cum, 0, 20 * nl), part(pen, 0, 20 * nl), Op.max)
        if more:
            ts(og, part(cum, 20 * nl, 20 * lists), -1.0, Op.mult)
            act(vw("OLN", 0, C), ind(vw("J128", 0, 144), og), Act.Copy)
        if t > 0:
            tt(mn1, part(tmx, 0, 20), part(tmx, 20, 40), Op.min)
            low = mn1
        if t > 1:
            tt(mn2, mn1, part(tmx, 40, 60), Op.min)
            low = mn2
        tt(place, low, bgo, Op.max)
        cp(pu, place)
        act(sgn, place, Act.Sign, bias=-127.5)
        lin(chk, sgn, (HB[t] - 128) / 2, (HB[t] - 128) / 2)
        if t > 0:
            lin(ch3, sgn, 160.0, 160.0)
        scatter(vw("PL", 0, C), pu, vw("PAY", 0, C))
        if more:
            count(0)
            count(1)
        tt(lv[nl], lv[t], ch3 if t else chk, Op.add)
        if more:
            act(part(pen, 0, 20), lv[nl], Act.Relu, bias=-319.0 * BIG, scale=BIG)
            act(part(pen, 20 * nl, 20 * nl + 20), lv[nl], Act.Relu, bias=320.0 * nl * BIG, scale=-BIG)
            if t == 1:
                act(p02, lv[nl], Act.Abs, bias=-479.5)
                act(part(pen, 20, 40), p02, Act.Relu, bias=-159.5 * BIG, scale=BIG)
            count(2)
        scan(vw("CZ", 0, 192), vw("C4", 0, 192), vw("PL", 128, C), 0.0, Op.add, Op.max)
        tt(npt, chk, place, Op.add)
        ts(vi, vw("CZ", 3, 192, 4), n4, Op.add)
        cp(olv, lv[nl])
        ts(ei, vi, 11, Op.logical_shift_right, 4092, Op.bitwise_and)
        ts(ri, vi, 1023, Op.bitwise_and)
        ts(oo, ei, pt, Op.add)
        ts(ord_, ri, 4.0, Op.mult, pt2, Op.add)
        for k in range(3):
            act(vw("OWN", 256 * k, 256 * k + 256), ind(X[t], part(oo, 16 * k, 16 * k + 16)), Act.Copy, scale=0.5)
        tt(ptr[nl], ptr[t], npt, Op.max)
        if more:
            tt(uk, ptr[nl], kc, Op.add)
            ts(ox, ptr[nl], -float(XB), Op.add)
            for l in range(1, nl + 1):
                tt(part(kraw, 20 * l - 20, 20 * l), uk, part(pen, 20 * l, 20 * l + 20), Op.subtract)
            if t == 0:
                tt(part(kold, 0, 20), part(kraw, 0, 20), bc, Op.max)
            else:
                tt(knew, kraw, kold, Op.max)
        else:
            quant("V", 0, 128, vw("VB", 0, 512))
            ts(ox, ptr[nl], -float(XB), Op.add)
            act(vw("OLN", 0, C), ind(vw("LT", 0, 1280), olv), Act.Copy)
            dma("y", [vw("OLN", 0, C)], [], T.ol[:], T.OLN[0:128:16, :])
        seen = vw("STH", 0, 4 * (HB[t] - E))
        for k in range(3):
            tt(vw("Z", 256 * k, 256 * k + 256), ind(seen, part(ord_, 16 * k, 16 * k + 16)), vw("OWN", 256 * k, 256 * k + 256), Op.add)
            if k == 0 and more:
                cp(part(okey, 0, 20 * nl), part(knew if t else kold, 0, 20 * nl))
                count(3)
                for b in range(4):
                    lin(part(ot4, 4 * b, 4 * b + 4), gsum, -2.0, 640.0 + b)
                keys(1)
        quant("Z", 0, 192, vw("Z", 0, 768))
        for b in range(4):
            mm(4 + b, "W", 128 * b, "Z", 0, 192)
        if more:
            cp(ot, ot4)
        seen = HB[t] + 192 - XB
        for b in range(4):
            if b % 2 == 0:
                ts(plane(b, HB[t], 192), vw("P%d" % (4 + b), 0, 192), 0.03125, Op.mult)
                cp(vw(X[nl][0], b, 4 * C, 4), ind(plane(b, XB, seen), ox))
            else:
                act(plane(b, HB[t], 192), vw("P%d" % (4 + b), 0, 192), Act.Copy, scale=0.03125)
                k = 14 if b == 3 else 20
                act(vw(X[nl][0], b, 64 * k, 4), ind(plane(b, XB, seen), part(ox, 0, k)), Act.Copy)
        cp(vw(X[nl][0], 64 * 14 + 3, 4 * C, 4), ind(plane(3, XB, seen), part(ox, 14, 20)))

    quant("X3", 0, C, X[R])
    mm(0, "V", 0, "X3", 0, 160)
    mm(1, "V", 0, "X3", 160, 160)
    dma("y", [vw("qX3", 0, C)], [], T.oc[:], T.qX3[:].bitcast(dt.uint8))
    for k in range(4):
        dma("y", [vw("sX3", 0, C)], [], T.osc[4 * k:4 * k + 4, :], T.sX3[32 * k:32 * k + 4, :])
    cp(vw("YB", 0, 160), vw("P0", 0, 160))
    act(vw("YB", 160, C), vw("P1", 0, 160), Act.Copy)
    dma("y", [vw("YB", 0, 160)], [], T.y[:, 0:160], T.YB[:, 0:160])
    dma("s", [vw("YB", 160, C)], [], T.y[:, 160:C], T.YB[:, 160:C])

    emit_all(ops, {"v": g.vector, "s": g.scalar, "t": g.tensor, "g": g, "y": g.sync}, T)
    g.wait_ge(T.sem.sent, used["sent"])
